import numpy as np
import ml_dtypes


def mxq(x, axis, fmt="e4m3"):
    dtype, down = {"e4m3": (ml_dtypes.float8_e4m3fn, 7), "e5m2": (ml_dtypes.float8_e5m2, 14)}[fmt]
    v = np.moveaxis(np.asarray(x, np.float32).astype(ml_dtypes.bfloat16).astype(np.float64), axis, -1)
    blocks = v.reshape(v.shape[:-1] + (-1, 32))
    amax = np.abs(blocks).max(-1, keepdims=True)
    byte = np.maximum(np.where(amax > 0, np.frexp(amax)[1] - 1 + 127, 0) - down, 1)
    scale = np.exp2(byte - 127.0)
    codes = (blocks / scale).astype(np.float32).astype(dtype).astype(np.float64)
    return np.moveaxis((codes * scale).reshape(v.shape), -1, axis)


WIDE = False


def mx_kscale(k):
    if not WIDE:
        return np.ones(k)
    levels = np.array([10, -10, 5, -5, 0])
    if k % 512:
        return np.exp2(np.random.permutation(np.resize(levels, k // 32))).repeat(32)
    a = np.empty((k // 512, 16))
    for p in range(k // 512):
        a[p, :8] = np.random.permutation(np.resize(levels, 8))
        for g in range(8):
            far = levels[np.abs(levels - a[p, g]) >= 10]
            a[p, g + 8] = far[np.random.randint(len(far))]
    return np.exp2(a.ravel()).repeat(32)


BF16 = ml_dtypes.bfloat16


def bf(x):
    return np.asarray(x, np.float32).astype(BF16)


def f64(x):
    return np.asarray(x).astype(np.float64)

def planes(Y):
    n, m = Y.shape
    b = f64(bf(Y)).reshape(n // 32, 32, m)
    amax = np.abs(b).max(1)
    byte = np.clip(np.where(amax > 0, np.frexp(amax)[1] - 1 + 127 - 7, 1), 1, 254)
    codes = (b * np.exp2(127.0 - byte)[:, None, :]).reshape(n, m).astype(np.float32).astype(ml_dtypes.float8_e4m3fn).view(np.uint8)
    words = codes.reshape(n // 512, 128, 4, m).transpose(0, 1, 3, 2)
    return np.ascontiguousarray(words), np.ascontiguousarray(byte.astype(np.uint8).reshape(n // 512, 16, m))


S, K, M = 1024, 1024, 1024


def psi(t):
    return t * np.abs(t)


def setup_inputs():
    s, t = mx_kscale(K), mx_kscale(M)
    row = np.exp(0.2 * np.random.standard_normal((S, 1)))
    x = np.random.standard_normal((S, K)) * row / s[None, :]
    a = np.random.standard_normal((M, K)) / np.sqrt(K) * t[:, None] * s[None, :]
    w = (1.0 + 0.1 * np.random.standard_normal(M)) / t**3
    d = 0.01 * np.sqrt(K / M) * (1.0 + 0.1 * np.random.standard_normal(K)) / s
    return {"x": bf(x), "a": bf(a), "w": bf(w), "d": bf(d)}


def core(x, a, w, d):
    af = f64(a)
    y = mxq(f64(x), 1, "e4m3") @ mxq(af, 1, "e4m3").T
    u = f64(w)[None, :] * y * np.abs(y)
    t = mxq(u, 1, "e4m3") @ mxq(af, 0, "e4m3")
    z = f64(d)[None, :] * t
    az = np.abs(z)
    cube_mean = np.mean(az * az * az, axis=-1, keepdims=True)
    nrm = np.power(cube_mean + 1e-6, 2.0 / 3.0)
    return psi(z) / nrm


def reference(x, a, w, d):
    R_out = core(x, a, w, d)
    words, scales = planes(R_out.T)
    return R_out, words, scales

@@ -1,0 +1,508 @@
+from contextlib import ExitStack
+
+import concourse.mybir as mybir
+from concourse.masks import make_identity
+
+S, K, M = 1024, 1024, 1024
+FLOPS = 2 * S * K * M * 2
+
+F32 = mybir.dt.float32
+BF16 = mybir.dt.bfloat16
+U32 = mybir.dt.uint32
+I32 = mybir.dt.int32
+U8 = mybir.dt.uint8
+FP8X4 = mybir.dt.float8_e4m3fn_x4
+ACT = mybir.ActivationFunctionType
+ALU = mybir.AluOpType
+
+P = 128
+PACK = 4
+BANK = 512
+GROUPS = 2
+TILES = 8
+EPS = 1e-6
+CHUNKS = [256, 256, 256, 128, 128]
+LAG = 3
+TAIL = 0.9
+W_S, Q_S, X_T, X_E, X_Q, D_SQ, D_CUBE = 1.61, 1.51, 0.21, 1.01, 0.71, 1.61, 0.51
+D_NORM, D_OUT, D_ROUND, D_ROWS, D_EMPTY, D_PLANES = 0.91, 2.31, 3.61, 4.81, 5.71, 6.91
+BANKS = {"y": 2, "t": 2, "turn": 4}
+WEAVE_U = ["scalar"] * 4 + ["vector"] * 6
+ROUND = ["vector"] * 7 + ["split"]
+
+
+def tile_weightedsignedsquarepowerstep_kernel(tc, x, a, w, d, out_0, out_1, out_2):
+    nc = tc.nc
+    starts = [sum(CHUNKS[:c]) for c in range(len(CHUNKS))]
+
+    with ExitStack() as ctx:
+        keep = ctx.enter_context(tc.tile_pool(name="keep", bufs=1))
+        work = ctx.enter_context(tc.tile_pool(name="work", bufs=2))
+        psum = ctx.enter_context(tc.psum_pool(name="psum", bufs=8))
+        ctx.enter_context(tc.manual_schedule())
+
+        def new_bank(role):
+            return psum.tile([P, BANK], F32, name=role, bufs=BANKS[role])
+
+        def copy_on(engine, out, in_):
+            if engine == "scalar":
+                nc.scalar.copy(out=out, in_=in_)
+            else:
+                nc.vector.tensor_copy(out=out, in_=in_)
+
+        def quantize(codes, scales, values):
+            nc.vector.quantize_mx(out=codes.bitcast(FP8X4), scales=scales, in_=values)
+
+        def mx_tiles(pool, name, words, bufs=None):
+            codes = pool.tile([P, words], U32, name=name + "_codes", align_bytes=64, bufs=bufs)
+            scales = pool.tile([P, words], U8, name=name + "_scales", align_bytes=64, bufs=bufs)
+            return codes, scales
+
+        def mx_product(out, left, left_cols, right, right_cols):
+            for g in range(GROUPS):
+                nc.tensor.matmul_mx(
+                    out=out,
+                    lhsT=left[g][0][:, left_cols[g]].bitcast(FP8X4),
+                    lhsT_scale=left[g][1][:, left_cols[g]],
+                    rhs=right[g][0][:, right_cols[g]].bitcast(FP8X4),
+                    rhs_scale=right[g][1][:, right_cols[g]],
+                    start=(g == 0),
+                    stop=(g == GROUPS - 1),
+                )
+
+        a_parts = a.rearrange("(g p j) (h k) -> g h p j k", g=GROUPS, j=PACK, h=GROUPS)
+        a_sb = {}
+        for g in range(GROUPS):
+            for h in range(GROUPS):
+                a_sb[g, h] = keep.tile([P, PACK * BANK], BF16, name="a_sb%d%d" % (g, h), align_bytes=256)
+        x_sb = [keep.tile([P, K], BF16, name="x_sb%d" % t, align_bytes=256) for t in range(S // P)]
+        w_bf = keep.tile([P, TILES], BF16, name="w_bf")
+        d_bf = keep.tile([TILES, P], BF16, name="d_bf")
+
+        def load_x(t):
+            nc.sync.dma_start(out=x_sb[t][:], in_=x[t * P : (t + 1) * P, :])
+
+        def load_a(g, h):
+            nc.sync.dma_start(out=a_sb[g, h][:].rearrange("p (j k) -> p j k", j=PACK), in_=a_parts[g][h])
+
+        first_tiles = CHUNKS[0] // P
+        load_a(0, 0)
+        load_x(0)
+        load_a(0, 1)
+        for t in range(1, first_tiles):
+            load_x(t)
+        nc.sync.dma_start(out=w_bf[:].rearrange("p (g j) -> p g j", j=PACK), in_=w.rearrange("(g p j) -> p g j", g=GROUPS, j=PACK))
+        nc.sync.dma_start(out=d_bf[:], in_=d.rearrange("(i p) -> i p", p=P))
+        load_a(1, 0)
+        load_a(1, 1)
+        for t in range(first_tiles, S // P):
+            load_x(t)
+
+        ident = keep.tile([P, P], F32, name="ident")
+        make_identity(nc, ident[:])
+        ones = keep.tile([P, 1], F32, name="ones")
+        nc.vector.memset(ones[:], 1.0)
+        power = keep.tile([P, 1], F32, name="power")
+        nc.scalar.activation(out=power[:], in_=ones[:], func=ACT.Identity, scale=-2.0 / 3.0)
+        d_square = keep.tile([P, P], F32, name="d_square")
+        nc.gpsimd.memset(d_square[:], 0.0)
+        w_col = keep.tile([P, TILES], F32, name="w_col")
+        d_col = keep.tile([P, TILES], F32, name="d_col")
+
+        def gains():
+            nc.gpsimd.tensor_copy(out=w_col[:], in_=w_bf[:])
+            nc.gpsimd.tensor_copy(out=d_square[0:TILES, :], in_=d_bf[:])
+
+        turned = {}
+
+        def turn_d():
+            turned["d"] = new_bank("turn")
+            nc.tensor.transpose(turned["d"][:, 0:P], d_square[:], ident[:])
+
+        def empty_d():
+            nc.scalar.copy(out=d_col[:], in_=turned["d"][:, 0:TILES])
+
+        def turn_words(key, sources):
+            bank = turned[key] = new_bank("turn")
+            for e, source in enumerate(sources):
+                nc.tensor.transpose(bank[:, e * P : (e + 1) * P], source, ident[:])
+
+        def every_second(words):
+            return [words[:, 2 * P * b + u : 2 * P * (b + 1) : 2] for b in range(2) for u in range(2)]
+
+        def empty_words(key, engine, staged):
+            blocks = staged.shape[1]
+            copy_on(engine, staged, turned[key][:, 0 : blocks * 2 * P].rearrange("p (b u r) -> p b r u", b=blocks, u=2))
+
+        def staged_words(tile, rows):
+            return tile[:].bitcast(F32).rearrange("p (h r u) -> p h r u", h=GROUPS, u=2)[:, :, rows, :]
+
+        a1 = [mx_tiles(keep, "a1_%d" % pair, 2 * GROUPS * P) for pair in range(TILES // 2)]
+        a1_in = {}
+
+        def turn_a(pair, h):
+            words = a_sb[pair // 2, h][:].bitcast(F32)
+            turn_words(("a", pair, h), every_second(words[:, pair % 2 * BANK : (pair % 2 + 1) * BANK]))
+
+        def empty_a(pair, h, engine):
+            a1_in[pair, h] = work.tile([P, 2 * P * PACK], BF16, name="a1_in", align_bytes=64, bufs=3)
+            empty_words(("a", pair, h), engine, staged_words(a1_in[pair, h], slice(0, P)))
+
+        def quantize_a1(pair, h):
+            cols = slice(h * 2 * P, (h + 1) * 2 * P)
+            quantize(a1[pair][0][:, cols], a1[pair][1][:, cols], a1_in[pair, h][:])
+
+        x_in, xq = {}, {}
+
+        def turn_x(c, t):
+            turn_words(("x", c, t), every_second(x_sb[starts[c] // P + t][:].bitcast(F32)))
+
+        def empty_x(c, t, engine):
+            if t == 0:
+                x_in[c] = work.tile([P, GROUPS * CHUNKS[c] * PACK], BF16, name="x_in", align_bytes=64)
+            empty_words(("x", c, t), engine, staged_words(x_in[c], slice(t * P, (t + 1) * P)))
+
+        def quantize_x(c):
+            xq[c] = mx_tiles(work, "xq", GROUPS * CHUNKS[c])
+            quantize(xq[c][0][:], xq[c][1][:], x_in[c][:])
+
+        a2 = [mx_tiles(keep, "a2_%d" % g, K) for g in range(GROUPS)]
+        a2_in = {}
+
+        def interleave(engine, out, in_):
+            if engine == "gpsimd":
+                nc.gpsimd.tensor_scalar(
+                    out=out.rearrange("p (s j) -> p s j", j=PACK),
+                    in0=in_.rearrange("p j s -> p s j"),
+                    scalar1=1.0,
+                    scalar2=0.0,
+                    op0=ALU.mult,
+                    op1=ALU.add,
+                )
+                return
+            copy_on(
+                engine,
+                out.rearrange("p (c i j) -> p c j i", i=4, j=PACK),
+                in_.rearrange("p j (c i) -> p c j i", i=4),
+            )
+
+        def weave_a(g, h, engine):
+            a2_in[g, h] = work.tile([P, BANK * PACK], BF16, name="a2_in", align_bytes=64)
+            interleave(engine, a2_in[g, h][:], a_sb[g, h][:].rearrange("p (j k) -> p j k", j=PACK))
+
+        def quantize_a2(g, h):
+            cols = slice(h * BANK, (h + 1) * BANK)
+            quantize(a2[g][0][:, cols], a2[g][1][:, cols], a2_in[g, h][:])
+
+        y_bank, y_abs, u_rows, u_in, uq = {}, {}, {}, {}, {}
+
+        def matmul_y(c, first):
+            n = CHUNKS[c]
+            y_bank[c, first] = new_bank("y")
+            for e in range(BANK // n):
+                i = first + e
+                mx_product(
+                    y_bank[c, first][:, e * n : (e + 1) * n],
+                    [a1[i // 2]] * GROUPS,
+                    [slice((h * 2 + i % 2) * P, (h * 2 + i % 2 + 1) * P) for h in range(GROUPS)],
+                    [xq[c]] * GROUPS,
+                    [slice(h * n, (h + 1) * n) for h in range(GROUPS)],
+                )
+
+        def abs_y(c, first):
+            y_abs[c, first] = work.tile([P, BANK], F32, name="y_abs")
+            nc.scalar.activation(out=y_abs[c, first][:], in_=y_bank[c, first][:], func=ACT.Abs)
+
+        def make_u(c, first):
+            n = CHUNKS[c]
+            for e in range(BANK // n):
+                i = first + e
+                if i % PACK == 0:
+                    u_rows[c, i // PACK] = work.tile([P, PACK * n], BF16, name="u_rows")
+                nc.vector.scalar_tensor_tensor(
+                    out=u_rows[c, i // PACK][:, i % PACK * n : (i % PACK + 1) * n],
+                    in0=y_bank[c, first][:, e * n : (e + 1) * n],
+                    scalar=w_col[:, i : i + 1],
+                    in1=y_abs[c, first][:, e * n : (e + 1) * n],
+                    op0=ALU.mult,
+                    op1=ALU.mult,
+                )
+
+        def weave_u(c, g, engine):
+            u_in[c, g] = work.tile([P, PACK * CHUNKS[c]], BF16, name="u_in", align_bytes=64)
+            interleave(engine, u_in[c, g][:], u_rows[c, g][:].rearrange("p (j s) -> p j s", j=PACK))
+
+        def quantize_u(c, g):
+            uq[c, g] = mx_tiles(work, "uq", CHUNKS[c], bufs=6)
+            quantize(uq[c, g][0][:], uq[c, g][1][:], u_in[c, g][:])
+
+        t_bank, z_abs, square, cube = {}, {}, {}, {}
+
+        def matmul_t(c, first):
+            n = CHUNKS[c]
+            t_bank[c, first] = new_bank("t")
+            for e in range(BANK // n):
+                i = first + e
+                mx_product(
+                    t_bank[c, first][:, e * n : (e + 1) * n],
+                    a2,
+                    [slice(i * P, (i + 1) * P)] * GROUPS,
+                    [uq[c, g] for g in range(GROUPS)],
+                    [slice(0, n)] * GROUPS,
+                )
+
+        def abs_z(c, first):
+            n = CHUNKS[c]
+            z_abs[c, first] = work.tile([P, BANK], F32, name="z_abs")
+            for e in range(BANK // n):
+                cols = slice(e * n, (e + 1) * n)
+                nc.scalar.activation(
+                    out=z_abs[c, first][:, cols],
+                    in_=t_bank[c, first][:, cols],
+                    func=ACT.Abs,
+                    scale=d_col[:, first + e : first + e + 1],
+                )
+
+        def powers_z(c, first):
+            n = CHUNKS[c]
+            if first == 0:
+                square[c] = work.tile([P, TILES * n], F32, name="square", bufs=3)
+                cube[c] = work.tile([P, TILES * n], F32, name="cube", bufs=3)
+            for result, factor, base in ((square[c], z_abs[c, first], 0), (cube[c], square[c], first * n)):
+                for e in range(BANK // n):
+                    i = first + e
+                    nc.vector.scalar_tensor_tensor(
+                        out=result[:, i * n : (i + 1) * n],
+                        in0=t_bank[c, first][:, e * n : (e + 1) * n],
+                        scalar=d_col[:, i : i + 1],
+                        in1=factor[:, base + e * n : base + (e + 1) * n],
+                        op0=ALU.mult,
+                        op1=ALU.mult,
+                    )
+
+        inv_norm = {}
+
+        def add_cubes(c, t, first, count):
+            n = CHUNKS[c]
+            if first == 0:
+                turned["cube", c, t] = new_bank("y" if count < TILES else "turn")
+            for i in range(first, first + count):
+                nc.tensor.matmul(
+                    out=turned["cube", c, t][:, 0:P],
+                    lhsT=cube[c][:, i * n + t * P : i * n + (t + 1) * P],
+                    rhs=ident[:],
+                    start=(i == 0),
+                    stop=(i == TILES - 1),
+                    is_transpose=True,
+                )
+
+        def norm(c, t):
+            terms = work.tile([P, P], F32, name="terms")
+            mean = work.tile([P, 1], F32, name="mean")
+            nc.scalar.activation(
+                out=terms[:],
+                in_=turned["cube", c, t][:, 0:P],
+                func=ACT.Identity,
+                scale=1.0 / K,
+                bias=EPS / P,
+                accum_out=mean[:],
+            )
+            inv_norm[c, t] = work.tile([P, 1], F32, name="inv_norm", bufs=3)
+            nc.gpsimd.tensor_tensor(out=inv_norm[c, t][:], in0=mean[:], in1=power[:], op=ALU.pow)
+
+        result, result_bf, plane_in = {}, {}, {}
+        plane_codes, plane_scales = mx_tiles(keep, "plane", GROUPS * S)
+
+        def turn_square(c, t, h, role):
+            n = CHUNKS[c]
+            bank = turned["square", c, t, h] = new_bank(role)
+            for e in range(PACK):
+                i = h * PACK + e
+                nc.tensor.transpose(bank[:, e * P : (e + 1) * P], square[c][:, i * n + t * P : i * n + (t + 1) * P], ident[:])
+
+        def scale_out(engine, out, in_, factor):
+            if engine == "scalar":
+                nc.scalar.activation(out=out, in_=in_, func=ACT.Copy, scale=factor)
+            else:
+                nc.vector.tensor_scalar(out=out, in0=in_, scalar1=factor, scalar2=None, op0=ALU.mult)
+
+        def finish_half(c, t, h, engine, also_round):
+            cols = slice(h * BANK, (h + 1) * BANK)
+            bank = turned["square", c, t, h]
+            if h == 0:
+                result[c, t] = work.tile([P, K], F32, name="result", bufs=3, align_bytes=256)
+            if also_round:
+                if h == 0:
+                    result_bf[c, t] = work.tile([P, K], BF16, name="result_bf")
+                scale_out(
+                    engine,
+                    result_bf[c, t][:, cols].rearrange("p (u r e) -> p u r e", u=2, e=2),
+                    bank[:].rearrange("p (r u e) -> p u r e", u=2, e=2),
+                    inv_norm[c, t][:],
+                )
+            scale_out(engine, result[c, t][:, cols], bank[:], inv_norm[c, t][:])
+
+        def store_rows(c, t, cols):
+            row = starts[c] + t * P
+            nc.sync.dma_start(out=out_0[row : row + P, cols], in_=result[c, t][:, cols])
+
+        def round_rows(c, t, engine):
+            result_bf[c, t] = work.tile([P, K], BF16, name="result_bf")
+            if engine == "gpsimd":
+                for h in range(GROUPS):
+                    cols = slice(h * BANK, (h + 1) * BANK)
+                    nc.gpsimd.tensor_scalar(
+                        out=result_bf[c, t][:, cols].rearrange("p (u r e) -> p u r e", u=2, e=2),
+                        in0=result[c, t][:, cols].rearrange("p (r u e) -> p u r e", u=2, e=2),
+                        scalar1=1.0,
+                        scalar2=0.0,
+                        op0=ALU.mult,
+                        op1=ALU.add,
+                    )
+                return
+            nc.vector.tensor_copy(
+                out=result_bf[c, t][:].rearrange("p (h u r e) -> p h u r e", h=GROUPS, u=2, e=2),
+                in_=result[c, t][:].rearrange("p (h r u e) -> p h u r e", h=GROUPS, u=2, e=2),
+            )
+
+        def turn_rows(c, t, first, count):
+            words = result_bf[c, t][:].bitcast(F32)
+            turn_words(("rows", c, t, first), [words[:, e * P : (e + 1) * P] for e in range(2 * first, 2 * (first + count))])
+
+        def empty_rows(c, t, first, count, engine):
+            if t == 0 and first == 0:
+                plane_in[c] = work.tile([P, GROUPS * CHUNKS[c] * PACK], BF16, name="plane_in", align_bytes=64)
+            staged = staged_words(plane_in[c], slice(t * P, (t + 1) * P))
+            empty_words(("rows", c, t, first), engine, staged[:, first : first + count, :, :])
+
+        def store_planes(c):
+            n = CHUNKS[c]
+            for h in range(GROUPS):
+                cols = slice(h * S + starts[c], h * S + starts[c] + n)
+                quantize(plane_codes[:, cols], plane_scales[:, cols], plane_in[c][:, h * n * PACK : (h + 1) * n * PACK])
+            rows = slice(starts[c], starts[c] + n)
+            nc.sync.dma_start(
+                out=out_1.rearrange("h p s t -> p h (s t)").bitcast(I32)[:, :, rows],
+                in_=plane_codes[:].bitcast(I32).rearrange("p (h s) -> p h s", h=GROUPS)[:, :, rows],
+            )
+
+        def store_scales(first, last, queues):
+            words = slice(first // 4, last // 4)
+            for quad in range(4):
+                queue = queues[quad % len(queues)]
+                queue.dma_start(
+                    out=out_2.bitcast(I32)[:, 4 * quad : 4 * quad + 4, words].rearrange("h r s -> r h s"),
+                    in_=plane_scales[32 * quad : 32 * quad + 4, :].bitcast(I32).rearrange("p (h s) -> p h s", h=GROUPS)[:, :, words],
+                )
+
+        plan = []
+
+        def at(time, call, *args):
+            plan.append((time, len(plan), call, args))
+
+        units = [TILES * n // BANK for n in CHUNKS]
+        second = [units[0] - 1 + LAG + sum(units[:c]) for c in range(len(CHUNKS))]
+        begin = [second[c] - units[c] - LAG + 1 for c in range(len(CHUNKS))]
+        both = begin[-1] + units[-1]
+
+        def clock(step):
+            return 2.0 * step if step <= both else 2.0 * both + TAIL * (step - both)
+
+        for c, n in enumerate(CHUNKS):
+            per_bank = BANK // n
+            tiles = n // P
+            last = c == len(CHUNKS) - 1
+            if c > 0:
+                for t in range(tiles):
+                    at(clock(begin[c] - 2 - tiles + t) + X_T, turn_x, c, t)
+                    at(clock(begin[c] - 2 - tiles + t) + X_E, empty_x, c, t, "scalar")
+                at(clock(begin[c] - 2) + X_Q, quantize_x, c)
+            for e in range(units[c]):
+                first, step = e * per_bank, begin[c] + e
+                at(clock(step - 1), matmul_y, c, first)
+                at(clock(step - 1) + 0.5, abs_y, c, first)
+                at(clock(step), make_u, c, first)
+                if (first + per_bank) % PACK == 0:
+                    how = WEAVE_U[2 * c + first // PACK]
+                    if how == "vector":
+                        at(clock(step) + 1.3, weave_u, c, first // PACK, how)
+                        at(clock(step + 1) + 0.3, quantize_u, c, first // PACK)
+                    else:
+                        at(clock(step) + W_S, weave_u, c, first // PACK, how)
+                        at(clock(step + 1) + Q_S, quantize_u, c, first // PACK)
+                step = second[c] + e
+                at(clock(step - 1) + 0.05, matmul_t, c, first)
+                at(clock(step - 1) + 0.55, abs_z, c, first)
+                at(clock(step) + 0.4, powers_z, c, first)
+                if last:
+                    at(clock(step + 1) + 0.1, turn_square, c, 0, e, "t")
+                    at(clock(step + 1) + (0.15 if e == 0 else 0.08), add_cubes, c, 0, first, per_bank)
+            done = second[c] + units[c]
+            for t in range(tiles):
+                now = clock(done + t)
+                how = ROUND[starts[c] // P + t]
+                if not last:
+                    at(now + D_CUBE, add_cubes, c, t, 0, TILES)
+                at(now + D_NORM, norm, c, t)
+                for h in range(GROUPS):
+                    if not last:
+                        at(now + D_SQ, turn_square, c, t, h, "turn")
+                    if how == "split":
+                        at(now + D_OUT, finish_half, c, t, h, ["scalar", "vector"][h], True)
+                        at(now + D_OUT, store_rows, c, t, slice(h * BANK, (h + 1) * BANK))
+                        at(now + D_ROUND, turn_rows, c, t, h, 1)
+                        at(now + D_ROWS, empty_rows, c, t, h, 1, ["scalar", "vector"][h])
+                    else:
+                        at(now + D_OUT, finish_half, c, t, h, "scalar", how == "scalar")
+                if how != "split":
+                    at(now + D_OUT, store_rows, c, t, slice(0, K))
+                    if how != "scalar":
+                        at(now + D_ROUND, round_rows, c, t, how)
+                    at(now + D_ROWS, turn_rows, c, t, 0, GROUPS)
+                    at(now + D_EMPTY, empty_rows, c, t, 0, GROUPS, "scalar")
+            at(now + D_PLANES, store_planes, c)
+            if last:
+                at(now + D_PLANES, store_scales, 0, S, [nc.scalar, nc.sync])
+
+        def prepare_a(pair, h):
+            turn_a(pair, h)
+            empty_a(pair, h, "scalar")
+
+        def prepare_x(t):
+            turn_x(0, t)
+            empty_x(0, t, "scalar")
+
+        weave_a(0, 0, "vector")
+        prepare_a(0, 0)
+        prepare_a(1, 0)
+        quantize_a2(0, 0)
+        quantize_a1(0, 0)
+        weave_a(0, 1, "vector")
+        prepare_x(0)
+        prepare_a(0, 1)
+        quantize_a1(1, 0)
+        quantize_a2(0, 1)
+        prepare_x(1)
+        prepare_a(1, 1)
+        gains()
+        quantize_a1(0, 1)
+        weave_a(1, 0, "vector")
+        quantize_x(0)
+        prepare_a(2, 0)
+        quantize_a1(1, 1)
+        quantize_a2(1, 0)
+        at(-1.9, turn_a, 2, 1)
+        at(-1.0, empty_a, 2, 1, "scalar")
+        at(-0.9, weave_a, 1, 1, "vector")
+        at(-0.8, quantize_a1, 2, 0)
+        at(-0.7, quantize_a2, 1, 1)
+        at(0.9, quantize_a1, 2, 1)
+        for h in range(GROUPS):
+            at(0.1, turn_a, 3, h)
+            at(0.9, empty_a, 3, h, "scalar")
+            at(3.5, quantize_a1, 3, h)
+        at(4.3, turn_d)
+        at(5.5, empty_d)
+
+        for time, number, call, args in sorted(plan, key=lambda entry: entry[:2]):
+            call(*args)

@@ -21,24 +21,20 @@ BANK = 512
 GROUPS = 2
 TILES = 8
 EPS = 1e-6
-CHUNKS = [256, 256, 256, 128, 128]
-LAG = 3
-TAIL = 0.9
-W_S, Q_S, X_T, X_E, X_Q, D_SQ, D_CUBE = 1.61, 1.51, 0.21, 1.01, 0.71, 1.61, 0.51
-D_NORM, D_OUT, D_ROUND, D_ROWS, D_EMPTY, D_PLANES = 0.91, 2.31, 3.61, 4.81, 5.71, 6.91
-BANKS = {"y": 2, "t": 2, "turn": 4}
-WEAVE_U = ["scalar"] * 4 + ["vector"] * 6
-ROUND = ["vector"] * 7 + ["split"]
+
+CHUNK = 256
+CHUNKS = S // CHUNK
+PIECES = [256, 256, 256, 128, 128]
+BANKS = {"y": 3, "t": 2, "turn": 3}
 
 
 def tile_weightedsignedsquarepowerstep_kernel(tc, x, a, w, d, out_0, out_1, out_2):
     nc = tc.nc
-    starts = [sum(CHUNKS[:c]) for c in range(len(CHUNKS))]
 
     with ExitStack() as ctx:
         keep = ctx.enter_context(tc.tile_pool(name="keep", bufs=1))
         work = ctx.enter_context(tc.tile_pool(name="work", bufs=2))
-        psum = ctx.enter_context(tc.psum_pool(name="psum", bufs=8))
+        psum = ctx.enter_context(tc.psum_pool(name="psum", bufs=1))
         ctx.enter_context(tc.manual_schedule())
 
         def new_bank(role):
@@ -50,459 +46,469 @@ def tile_weightedsignedsquarepowerstep_kernel(tc, x, a, w, d, out_0, out_1, out_
             else:
                 nc.vector.tensor_copy(out=out, in_=in_)
 
-        def quantize(codes, scales, values):
-            nc.vector.quantize_mx(out=codes.bitcast(FP8X4), scales=scales, in_=values)
+        def scale_on(engine, out, in_, factor):
+            if engine == "scalar":
+                nc.scalar.activation(out=out, in_=in_, func=ACT.Copy, scale=factor)
+            else:
+                nc.vector.tensor_scalar(out=out, in0=in_, scalar1=factor, scalar2=None, op0=ALU.mult)
 
-        def mx_tiles(pool, name, words, bufs=None):
+        def mx_tiles(pool, name, words, bufs):
             codes = pool.tile([P, words], U32, name=name + "_codes", align_bytes=64, bufs=bufs)
             scales = pool.tile([P, words], U8, name=name + "_scales", align_bytes=64, bufs=bufs)
             return codes, scales
 
-        def mx_product(out, left, left_cols, right, right_cols):
-            for g in range(GROUPS):
+        def quantize(operand, cols, values):
+            nc.vector.quantize_mx(out=operand[0][:, cols].bitcast(FP8X4), scales=operand[1][:, cols], in_=values)
+
+        def mx_product(out, passes):
+            for g, (left, left_cols, right, right_cols) in enumerate(passes):
                 nc.tensor.matmul_mx(
                     out=out,
-                    lhsT=left[g][0][:, left_cols[g]].bitcast(FP8X4),
-                    lhsT_scale=left[g][1][:, left_cols[g]],
-                    rhs=right[g][0][:, right_cols[g]].bitcast(FP8X4),
-                    rhs_scale=right[g][1][:, right_cols[g]],
+                    lhsT=left[0][:, left_cols].bitcast(FP8X4),
+                    lhsT_scale=left[1][:, left_cols],
+                    rhs=right[0][:, right_cols].bitcast(FP8X4),
+                    rhs_scale=right[1][:, right_cols],
                     start=(g == 0),
                     stop=(g == GROUPS - 1),
                 )
 
-        a_parts = a.rearrange("(g p j) (h k) -> g h p j k", g=GROUPS, j=PACK, h=GROUPS)
+        def part(index, width):
+            return slice(index * width, (index + 1) * width)
+
+        a_parts = a.rearrange("(g p j) (h c) -> g h p j c", g=GROUPS, j=PACK, h=GROUPS)
         a_sb = {}
         for g in range(GROUPS):
             for h in range(GROUPS):
                 a_sb[g, h] = keep.tile([P, PACK * BANK], BF16, name="a_sb%d%d" % (g, h), align_bytes=256)
-        x_sb = [keep.tile([P, K], BF16, name="x_sb%d" % t, align_bytes=256) for t in range(S // P)]
-        w_bf = keep.tile([P, TILES], BF16, name="w_bf")
-        d_bf = keep.tile([TILES, P], BF16, name="d_bf")
-
-        def load_x(t):
-            nc.sync.dma_start(out=x_sb[t][:], in_=x[t * P : (t + 1) * P, :])
+        x_sb = [keep.tile([P, K], BF16, name="x_sb%d" % t, align_bytes=256) for t in range(TILES)]
+        w_col = keep.tile([P, TILES], BF16, name="w_col")
+        d_rows = keep.tile([TILES, P], BF16, name="d_rows")
 
         def load_a(g, h):
-            nc.sync.dma_start(out=a_sb[g, h][:].rearrange("p (j k) -> p j k", j=PACK), in_=a_parts[g][h])
+            nc.sync.dma_start(out=a_sb[g, h][:].rearrange("p (j c) -> p j c", j=PACK), in_=a_parts[g][h])
 
-        first_tiles = CHUNKS[0] // P
-        load_a(0, 0)
-        load_x(0)
-        load_a(0, 1)
-        for t in range(1, first_tiles):
-            load_x(t)
-        nc.sync.dma_start(out=w_bf[:].rearrange("p (g j) -> p g j", j=PACK), in_=w.rearrange("(g p j) -> p g j", g=GROUPS, j=PACK))
-        nc.sync.dma_start(out=d_bf[:], in_=d.rearrange("(i p) -> i p", p=P))
-        load_a(1, 0)
-        load_a(1, 1)
-        for t in range(first_tiles, S // P):
+        def load_x(t):
+            nc.sync.dma_start(out=x_sb[t][:], in_=x[part(t, P), :])
+
+        for h in range(GROUPS):
+            load_a(0, h)
+            load_x(h)
+        for h in range(GROUPS):
+            load_a(1, h)
+        nc.sync.dma_start(
+            out=w_col[:].rearrange("p (g j) -> p g j", j=PACK),
+            in_=w.rearrange("(g p j) -> p g j", g=GROUPS, j=PACK),
+        )
+        load_x(2)
+        load_x(3)
+        nc.sync.dma_start(out=d_rows[:], in_=d.rearrange("(i p) -> i p", p=P))
+        for t in range(4, TILES):
             load_x(t)
 
         ident = keep.tile([P, P], F32, name="ident")
         make_identity(nc, ident[:])
-        ones = keep.tile([P, 1], F32, name="ones")
-        nc.vector.memset(ones[:], 1.0)
+        one = keep.tile([P, 1], F32, name="one")
+        nc.vector.memset(one[:], 1.0)
         power = keep.tile([P, 1], F32, name="power")
-        nc.scalar.activation(out=power[:], in_=ones[:], func=ACT.Identity, scale=-2.0 / 3.0)
+        nc.scalar.activation(out=power[:], in_=one[:], func=ACT.Identity, scale=-2.0 / 3.0)
         d_square = keep.tile([P, P], F32, name="d_square")
         nc.gpsimd.memset(d_square[:], 0.0)
-        w_col = keep.tile([P, TILES], F32, name="w_col")
         d_col = keep.tile([P, TILES], F32, name="d_col")
-
-        def gains():
-            nc.gpsimd.tensor_copy(out=w_col[:], in_=w_bf[:])
-            nc.gpsimd.tensor_copy(out=d_square[0:TILES, :], in_=d_bf[:])
 
         turned = {}
 
-        def turn_d():
-            turned["d"] = new_bank("turn")
-            nc.tensor.transpose(turned["d"][:, 0:P], d_square[:], ident[:])
-
-        def empty_d():
-            nc.scalar.copy(out=d_col[:], in_=turned["d"][:, 0:TILES])
-
-        def turn_words(key, sources):
-            bank = turned[key] = new_bank("turn")
+        def turn(key, sources, role):
+            turned[key] = new_bank(role)
             for e, source in enumerate(sources):
-                nc.tensor.transpose(bank[:, e * P : (e + 1) * P], source, ident[:])
+                nc.tensor.transpose(turned[key][:, part(e, P)], source, ident[:])
 
         def every_second(words):
             return [words[:, 2 * P * b + u : 2 * P * (b + 1) : 2] for b in range(2) for u in range(2)]
 
-        def empty_words(key, engine, staged):
-            blocks = staged.shape[1]
-            copy_on(engine, staged, turned[key][:, 0 : blocks * 2 * P].rearrange("p (b u r) -> p b r u", b=blocks, u=2))
+        def empty_words(key, engine, staged, rows):
+            copy_on(
+                engine,
+                staged[:].bitcast(F32).rearrange("p (b r u) -> p b r u", b=2, u=2)[:, :, rows, :],
+                turned[key][:].rearrange("p (b u r) -> p b r u", b=2, u=2),
+            )
 
-        def staged_words(tile, rows):
-            return tile[:].bitcast(F32).rearrange("p (h r u) -> p h r u", h=GROUPS, u=2)[:, :, rows, :]
-
-        a1 = [mx_tiles(keep, "a1_%d" % pair, 2 * GROUPS * P) for pair in range(TILES // 2)]
-        a1_in = {}
-
-        def turn_a(pair, h):
-            words = a_sb[pair // 2, h][:].bitcast(F32)
-            turn_words(("a", pair, h), every_second(words[:, pair % 2 * BANK : (pair % 2 + 1) * BANK]))
-
-        def empty_a(pair, h, engine):
-            a1_in[pair, h] = work.tile([P, 2 * P * PACK], BF16, name="a1_in", align_bytes=64, bufs=3)
-            empty_words(("a", pair, h), engine, staged_words(a1_in[pair, h], slice(0, P)))
-
-        def quantize_a1(pair, h):
-            cols = slice(h * 2 * P, (h + 1) * 2 * P)
-            quantize(a1[pair][0][:, cols], a1[pair][1][:, cols], a1_in[pair, h][:])
-
-        x_in, xq = {}, {}
-
-        def turn_x(c, t):
-            turn_words(("x", c, t), every_second(x_sb[starts[c] // P + t][:].bitcast(F32)))
-
-        def empty_x(c, t, engine):
-            if t == 0:
-                x_in[c] = work.tile([P, GROUPS * CHUNKS[c] * PACK], BF16, name="x_in", align_bytes=64)
-            empty_words(("x", c, t), engine, staged_words(x_in[c], slice(t * P, (t + 1) * P)))
-
-        def quantize_x(c):
-            xq[c] = mx_tiles(work, "xq", GROUPS * CHUNKS[c])
-            quantize(xq[c][0][:], xq[c][1][:], x_in[c][:])
-
-        a2 = [mx_tiles(keep, "a2_%d" % g, K) for g in range(GROUPS)]
-        a2_in = {}
-
-        def interleave(engine, out, in_):
-            if engine == "gpsimd":
-                nc.gpsimd.tensor_scalar(
-                    out=out.rearrange("p (s j) -> p s j", j=PACK),
-                    in0=in_.rearrange("p j s -> p s j"),
-                    scalar1=1.0,
-                    scalar2=0.0,
-                    op0=ALU.mult,
-                    op1=ALU.add,
-                )
-                return
+        def weave(engine, out, in_):
             copy_on(
                 engine,
                 out.rearrange("p (c i j) -> p c j i", i=4, j=PACK),
-                in_.rearrange("p j (c i) -> p c j i", i=4),
+                in_.rearrange("p (j c i) -> p c j i", i=4, j=PACK),
             )
 
-        def weave_a(g, h, engine):
-            a2_in[g, h] = work.tile([P, BANK * PACK], BF16, name="a2_in", align_bytes=64)
-            interleave(engine, a2_in[g, h][:], a_sb[g, h][:].rearrange("p (j k) -> p j k", j=PACK))
+        def turn_d():
+            nc.scalar.copy(out=d_square[0:TILES, :], in_=d_rows[:])
+            turn("d", [d_square[:]], "turn")
 
-        def quantize_a2(g, h):
-            cols = slice(h * BANK, (h + 1) * BANK)
-            quantize(a2[g][0][:, cols], a2[g][1][:, cols], a2_in[g, h][:])
+        def empty_d():
+            nc.scalar.copy(out=d_col[:], in_=turned["d"][:, 0:TILES])
 
-        y_bank, y_abs, u_rows, u_in, uq = {}, {}, {}, {}, {}
+        a_k = [mx_tiles(keep, "a_k%d" % pair, GROUPS * 2 * P, 1) for pair in range(TILES // 2)]
+        a_k_in, x_in, x_k = {}, {}, {}
 
-        def matmul_y(c, first):
-            n = CHUNKS[c]
-            y_bank[c, first] = new_bank("y")
-            for e in range(BANK // n):
-                i = first + e
-                mx_product(
-                    y_bank[c, first][:, e * n : (e + 1) * n],
-                    [a1[i // 2]] * GROUPS,
-                    [slice((h * 2 + i % 2) * P, (h * 2 + i % 2 + 1) * P) for h in range(GROUPS)],
-                    [xq[c]] * GROUPS,
-                    [slice(h * n, (h + 1) * n) for h in range(GROUPS)],
-                )
+        def turn_a(pair, h):
+            words = a_sb[pair // 2, h][:].bitcast(F32)
+            turn(("a", pair, h), every_second(words[:, part(pair % 2, BANK)]), "turn")
+            a_k_in[pair, h] = work.tile([P, 2 * P * PACK], BF16, name="a_k_in", align_bytes=64, bufs=4)
+            empty_words(("a", pair, h), "scalar", a_k_in[pair, h], slice(0, P))
 
-        def abs_y(c, first):
-            y_abs[c, first] = work.tile([P, BANK], F32, name="y_abs")
-            nc.scalar.activation(out=y_abs[c, first][:], in_=y_bank[c, first][:], func=ACT.Abs)
+        def quantize_a_k(pair, h):
+            quantize(a_k[pair], part(h, 2 * P), a_k_in[pair, h][:])
 
-        def make_u(c, first):
-            n = CHUNKS[c]
-            for e in range(BANK // n):
-                i = first + e
-                if i % PACK == 0:
-                    u_rows[c, i // PACK] = work.tile([P, PACK * n], BF16, name="u_rows")
+        def turn_x(t):
+            turn(("x", t), every_second(x_sb[t][:].bitcast(F32)), "turn")
+
+        def empty_x(t):
+            if t % 2 == 0:
+                x_in[t // 2] = work.tile([P, GROUPS * CHUNK * PACK], BF16, name="x_in", align_bytes=64)
+            empty_words(("x", t), "scalar", x_in[t // 2], part(t % 2, P))
+
+        def quantize_x(c):
+            x_k[c] = mx_tiles(keep, "x_k%d" % c, GROUPS * CHUNK, 1)
+            quantize(x_k[c], slice(0, GROUPS * CHUNK), x_in[c][:])
+
+        a_m = [mx_tiles(keep, "a_m%d" % g, K, 1) for g in range(GROUPS)]
+        a_m_in = {}
+
+        def weave_a(g, h):
+            a_m_in[g, h] = work.tile([P, BANK * PACK], BF16, name="a_m_in", align_bytes=64)
+            weave("vector", a_m_in[g, h][:], a_sb[g, h][:])
+
+        def quantize_a_m(g, h):
+            quantize(a_m[g], part(h, BANK), a_m_in[g, h][:])
+
+        y_bank, y_abs, u_slots, u_in, u_m = {}, {}, {}, {}, {}
+
+        def matmul_y(c, pair):
+            y_bank[c, pair] = new_bank("y")
+            for e in range(2):
+                passes = [(a_k[pair], part(2 * h + e, P), x_k[c], part(h, CHUNK)) for h in range(GROUPS)]
+                mx_product(y_bank[c, pair][:, part(e, CHUNK)], passes)
+
+        def abs_y(c, pair):
+            y_abs[c, pair] = work.tile([P, BANK], F32, name="y_abs", bufs=BANKS["y"] + 1)
+            nc.scalar.activation(out=y_abs[c, pair][:], in_=y_bank[c, pair][:], func=ACT.Abs)
+
+        def make_u(c, pair):
+            g = pair // 2
+            if pair % 2 == 0:
+                u_slots[c, g] = work.tile([P, PACK * CHUNK], BF16, name="u_slots", bufs=3)
+            for e in range(2):
+                i = 2 * pair + e
                 nc.vector.scalar_tensor_tensor(
-                    out=u_rows[c, i // PACK][:, i % PACK * n : (i % PACK + 1) * n],
-                    in0=y_bank[c, first][:, e * n : (e + 1) * n],
+                    out=u_slots[c, g][:, part(i % PACK, CHUNK)],
+                    in0=y_bank[c, pair][:, part(e, CHUNK)],
                     scalar=w_col[:, i : i + 1],
-                    in1=y_abs[c, first][:, e * n : (e + 1) * n],
+                    in1=y_abs[c, pair][:, part(e, CHUNK)],
                     op0=ALU.mult,
                     op1=ALU.mult,
                 )
 
         def weave_u(c, g, engine):
-            u_in[c, g] = work.tile([P, PACK * CHUNKS[c]], BF16, name="u_in", align_bytes=64)
-            interleave(engine, u_in[c, g][:], u_rows[c, g][:].rearrange("p (j s) -> p j s", j=PACK))
+            u_in[c, g] = work.tile([P, CHUNK * PACK], BF16, name="u_in", align_bytes=64, bufs=3)
+            weave(engine, u_in[c, g][:], u_slots[c, g][:])
 
         def quantize_u(c, g):
-            uq[c, g] = mx_tiles(work, "uq", CHUNKS[c], bufs=6)
-            quantize(uq[c, g][0][:], uq[c, g][1][:], u_in[c, g][:])
+            u_m[c, g] = mx_tiles(keep, "u_m%d%d" % (c, g), CHUNK, 1)
+            quantize(u_m[c, g], slice(0, CHUNK), u_in[c, g][:])
 
+        piece_start = [sum(PIECES[:q]) for q in range(len(PIECES))]
+        units = [(q, first) for q, n in enumerate(PIECES) for first in range(0, TILES, BANK // n)]
+        piece_of = [q for q, n in enumerate(PIECES) for t in range(n // P)]
         t_bank, z_abs, square, cube = {}, {}, {}, {}
 
-        def matmul_t(c, first):
-            n = CHUNKS[c]
-            t_bank[c, first] = new_bank("t")
+        def matmul_t(unit):
+            q, first = units[unit]
+            n, c, row = PIECES[q], piece_start[q] // CHUNK, piece_start[q] % CHUNK
+            t_bank[unit] = new_bank("t")
             for e in range(BANK // n):
-                i = first + e
-                mx_product(
-                    t_bank[c, first][:, e * n : (e + 1) * n],
-                    a2,
-                    [slice(i * P, (i + 1) * P)] * GROUPS,
-                    [uq[c, g] for g in range(GROUPS)],
-                    [slice(0, n)] * GROUPS,
-                )
+                passes = [(a_m[g], part(first + e, P), u_m[c, g], slice(row, row + n)) for g in range(GROUPS)]
+                mx_product(t_bank[unit][:, part(e, n)], passes)
 
-        def abs_z(c, first):
-            n = CHUNKS[c]
-            z_abs[c, first] = work.tile([P, BANK], F32, name="z_abs")
+        def abs_z(unit):
+            q, first = units[unit]
+            n = PIECES[q]
+            z_abs[unit] = work.tile([P, BANK], F32, name="z_abs")
             for e in range(BANK // n):
-                cols = slice(e * n, (e + 1) * n)
                 nc.scalar.activation(
-                    out=z_abs[c, first][:, cols],
-                    in_=t_bank[c, first][:, cols],
+                    out=z_abs[unit][:, part(e, n)],
+                    in_=t_bank[unit][:, part(e, n)],
                     func=ACT.Abs,
                     scale=d_col[:, first + e : first + e + 1],
                 )
 
-        def powers_z(c, first):
-            n = CHUNKS[c]
+        def times_z(unit, out, factor):
+            q, first = units[unit]
+            n = PIECES[q]
+            for e in range(BANK // n):
+                nc.vector.scalar_tensor_tensor(
+                    out=out[:, part(e, n)],
+                    in0=t_bank[unit][:, part(e, n)],
+                    scalar=d_col[:, first + e : first + e + 1],
+                    in1=factor[:, part(e, n)],
+                    op0=ALU.mult,
+                    op1=ALU.mult,
+                )
+
+        def powers_z(unit):
+            q, first = units[unit]
+            n = PIECES[q]
             if first == 0:
-                square[c] = work.tile([P, TILES * n], F32, name="square", bufs=3)
-                cube[c] = work.tile([P, TILES * n], F32, name="cube", bufs=3)
-            for result, factor, base in ((square[c], z_abs[c, first], 0), (cube[c], square[c], first * n)):
-                for e in range(BANK // n):
-                    i = first + e
-                    nc.vector.scalar_tensor_tensor(
-                        out=result[:, i * n : (i + 1) * n],
-                        in0=t_bank[c, first][:, e * n : (e + 1) * n],
-                        scalar=d_col[:, i : i + 1],
-                        in1=factor[:, base + e * n : base + (e + 1) * n],
-                        op0=ALU.mult,
-                        op1=ALU.mult,
-                    )
+                square[q] = work.tile([P, TILES * n], F32, name="square", bufs=3)
+                cube[q] = work.tile([P, TILES * n], F32, name="cube")
+            cols = slice(first * n, first * n + BANK)
+            times_z(unit, square[q][:, cols], z_abs[unit][:])
+            times_z(unit, cube[q][:, cols], square[q][:, cols])
+
+        def block(values, t, i):
+            q = piece_of[t]
+            start = i * PIECES[q] + t * P - piece_start[q]
+            return values[q][:, start : start + P]
 
         inv_norm = {}
 
-        def add_cubes(c, t, first, count):
-            n = CHUNKS[c]
+        def add_cubes(t, first, count, role):
             if first == 0:
-                turned["cube", c, t] = new_bank("y" if count < TILES else "turn")
+                turned["cube", t] = new_bank(role)
             for i in range(first, first + count):
                 nc.tensor.matmul(
-                    out=turned["cube", c, t][:, 0:P],
-                    lhsT=cube[c][:, i * n + t * P : i * n + (t + 1) * P],
+                    out=turned["cube", t][:, 0:P],
+                    lhsT=block(cube, t, i),
                     rhs=ident[:],
                     start=(i == 0),
                     stop=(i == TILES - 1),
                     is_transpose=True,
                 )
 
-        def norm(c, t):
+        def norm(t):
             terms = work.tile([P, P], F32, name="terms")
             mean = work.tile([P, 1], F32, name="mean")
             nc.scalar.activation(
                 out=terms[:],
-                in_=turned["cube", c, t][:, 0:P],
+                in_=turned["cube", t][:, 0:P],
                 func=ACT.Identity,
                 scale=1.0 / K,
                 bias=EPS / P,
                 accum_out=mean[:],
             )
-            inv_norm[c, t] = work.tile([P, 1], F32, name="inv_norm", bufs=3)
-            nc.gpsimd.tensor_tensor(out=inv_norm[c, t][:], in0=mean[:], in1=power[:], op=ALU.pow)
+            inv_norm[t] = work.tile([P, 1], F32, name="inv_norm", bufs=3)
+            nc.gpsimd.tensor_tensor(out=inv_norm[t][:], in0=mean[:], in1=power[:], op=ALU.pow)
 
-        result, result_bf, plane_in = {}, {}, {}
-        plane_codes, plane_scales = mx_tiles(keep, "plane", GROUPS * S)
+        result, rounded, out_in = {}, {}, {}
+        out_k = mx_tiles(keep, "out_k", GROUPS * S, 1)
 
-        def turn_square(c, t, h, role):
-            n = CHUNKS[c]
-            bank = turned["square", c, t, h] = new_bank(role)
-            for e in range(PACK):
-                i = h * PACK + e
-                nc.tensor.transpose(bank[:, e * P : (e + 1) * P], square[c][:, i * n + t * P : i * n + (t + 1) * P], ident[:])
-
-        def scale_out(engine, out, in_, factor):
-            if engine == "scalar":
-                nc.scalar.activation(out=out, in_=in_, func=ACT.Copy, scale=factor)
-            else:
-                nc.vector.tensor_scalar(out=out, in0=in_, scalar1=factor, scalar2=None, op0=ALU.mult)
-
-        def finish_half(c, t, h, engine, also_round):
-            cols = slice(h * BANK, (h + 1) * BANK)
-            bank = turned["square", c, t, h]
-            if h == 0:
-                result[c, t] = work.tile([P, K], F32, name="result", bufs=3, align_bytes=256)
-            if also_round:
-                if h == 0:
-                    result_bf[c, t] = work.tile([P, K], BF16, name="result_bf")
-                scale_out(
-                    engine,
-                    result_bf[c, t][:, cols].rearrange("p (u r e) -> p u r e", u=2, e=2),
-                    bank[:].rearrange("p (r u e) -> p u r e", u=2, e=2),
-                    inv_norm[c, t][:],
-                )
-            scale_out(engine, result[c, t][:, cols], bank[:], inv_norm[c, t][:])
-
-        def store_rows(c, t, cols):
-            row = starts[c] + t * P
-            nc.sync.dma_start(out=out_0[row : row + P, cols], in_=result[c, t][:, cols])
-
-        def round_rows(c, t, engine):
-            result_bf[c, t] = work.tile([P, K], BF16, name="result_bf")
-            if engine == "gpsimd":
-                for h in range(GROUPS):
-                    cols = slice(h * BANK, (h + 1) * BANK)
-                    nc.gpsimd.tensor_scalar(
-                        out=result_bf[c, t][:, cols].rearrange("p (u r e) -> p u r e", u=2, e=2),
-                        in0=result[c, t][:, cols].rearrange("p (r u e) -> p u r e", u=2, e=2),
-                        scalar1=1.0,
-                        scalar2=0.0,
-                        op0=ALU.mult,
-                        op1=ALU.add,
-                    )
-                return
-            nc.vector.tensor_copy(
-                out=result_bf[c, t][:].rearrange("p (h u r e) -> p h u r e", h=GROUPS, u=2, e=2),
-                in_=result[c, t][:].rearrange("p (h r u e) -> p h u r e", h=GROUPS, u=2, e=2),
-            )
-
-        def turn_rows(c, t, first, count):
-            words = result_bf[c, t][:].bitcast(F32)
-            turn_words(("rows", c, t, first), [words[:, e * P : (e + 1) * P] for e in range(2 * first, 2 * (first + count))])
-
-        def empty_rows(c, t, first, count, engine):
-            if t == 0 and first == 0:
-                plane_in[c] = work.tile([P, GROUPS * CHUNKS[c] * PACK], BF16, name="plane_in", align_bytes=64)
-            staged = staged_words(plane_in[c], slice(t * P, (t + 1) * P))
-            empty_words(("rows", c, t, first), engine, staged[:, first : first + count, :, :])
-
-        def store_planes(c):
-            n = CHUNKS[c]
+        def turn_square(t, role):
             for h in range(GROUPS):
-                cols = slice(h * S + starts[c], h * S + starts[c] + n)
-                quantize(plane_codes[:, cols], plane_scales[:, cols], plane_in[c][:, h * n * PACK : (h + 1) * n * PACK])
-            rows = slice(starts[c], starts[c] + n)
-            nc.sync.dma_start(
-                out=out_1.rearrange("h p s t -> p h (s t)").bitcast(I32)[:, :, rows],
-                in_=plane_codes[:].bitcast(I32).rearrange("p (h s) -> p h s", h=GROUPS)[:, :, rows],
+                turn(("square", t, h), [block(square, t, h * PACK + e) for e in range(PACK)], role)
+
+        def store_result(t, engines):
+            result[t] = work.tile([P, K], F32, name="result", bufs=3, align_bytes=256)
+            for h in range(GROUPS):
+                scale_on(engines[h], result[t][:, part(h, BANK)], turned["square", t, h][:], inv_norm[t][:])
+            nc.sync.dma_start(out=out_0[part(t, P), :], in_=result[t][:])
+
+        def round_result(t):
+            rounded[t] = work.tile([P, K], BF16, name="rounded")
+            nc.vector.tensor_copy(
+                out=rounded[t][:].rearrange("p (h u r e) -> p h u r e", h=GROUPS, u=2, e=2),
+                in_=result[t][:].rearrange("p (h r u e) -> p h u r e", h=GROUPS, u=2, e=2),
             )
 
-        def store_scales(first, last, queues):
-            words = slice(first // 4, last // 4)
-            for quad in range(4):
-                queue = queues[quad % len(queues)]
-                queue.dma_start(
-                    out=out_2.bitcast(I32)[:, 4 * quad : 4 * quad + 4, words].rearrange("h r s -> r h s"),
-                    in_=plane_scales[32 * quad : 32 * quad + 4, :].bitcast(I32).rearrange("p (h s) -> p h s", h=GROUPS)[:, :, words],
+        def round_from_psum(t, engines):
+            rounded[t] = work.tile([P, K], BF16, name="rounded")
+            for h in range(GROUPS):
+                scale_on(
+                    engines[h],
+                    rounded[t][:, part(h, BANK)].rearrange("p (u r e) -> p u r e", u=2, e=2),
+                    turned["square", t, h][:].rearrange("p (r u e) -> p u r e", u=2, e=2),
+                    inv_norm[t][:],
                 )
 
-        plan = []
+        def turn_rounded(t, role):
+            words = rounded[t][:].bitcast(F32)
+            turn(("rounded", t), [words[:, part(e, P)] for e in range(2 * GROUPS)], role)
 
-        def at(time, call, *args):
-            plan.append((time, len(plan), call, args))
+        def empty_rounded(t, engine):
+            q = piece_of[t]
+            row = t * P - piece_start[q]
+            if row == 0:
+                out_in[q] = work.tile([P, GROUPS * PIECES[q] * PACK], BF16, name="out_in", align_bytes=64, bufs=3)
+            empty_words(("rounded", t), engine, out_in[q], slice(row, row + P))
 
-        units = [TILES * n // BANK for n in CHUNKS]
-        second = [units[0] - 1 + LAG + sum(units[:c]) for c in range(len(CHUNKS))]
-        begin = [second[c] - units[c] - LAG + 1 for c in range(len(CHUNKS))]
-        both = begin[-1] + units[-1]
+        def store_codes(q):
+            rows = slice(piece_start[q], piece_start[q] + PIECES[q])
+            for h in range(GROUPS):
+                quantize(out_k, slice(h * S + rows.start, h * S + rows.stop), out_in[q][:, part(h, PIECES[q] * PACK)])
+            nc.sync.dma_start(
+                out=out_1.rearrange("h p s j -> p h (s j)").bitcast(I32)[:, :, rows],
+                in_=out_k[0][:].bitcast(I32).rearrange("p (h s) -> p h s", h=GROUPS)[:, :, rows],
+            )
 
-        def clock(step):
-            return 2.0 * step if step <= both else 2.0 * both + TAIL * (step - both)
+        def store_scales():
+            for quad in range(4):
+                queue = nc.scalar if quad % 2 == 0 else nc.sync
+                queue.dma_start(
+                    out=out_2.bitcast(I32)[:, part(quad, 4), :].rearrange("h r s -> r h s"),
+                    in_=out_k[1][32 * quad : 32 * quad + 4, :].bitcast(I32).rearrange("p (h s) -> p h s", h=GROUPS),
+                )
 
-        for c, n in enumerate(CHUNKS):
-            per_bank = BANK // n
-            tiles = n // P
-            last = c == len(CHUNKS) - 1
-            if c > 0:
-                for t in range(tiles):
-                    at(clock(begin[c] - 2 - tiles + t) + X_T, turn_x, c, t)
-                    at(clock(begin[c] - 2 - tiles + t) + X_E, empty_x, c, t, "scalar")
-                at(clock(begin[c] - 2) + X_Q, quantize_x, c)
-            for e in range(units[c]):
-                first, step = e * per_bank, begin[c] + e
-                at(clock(step - 1), matmul_y, c, first)
-                at(clock(step - 1) + 0.5, abs_y, c, first)
-                at(clock(step), make_u, c, first)
-                if (first + per_bank) % PACK == 0:
-                    how = WEAVE_U[2 * c + first // PACK]
-                    if how == "vector":
-                        at(clock(step) + 1.3, weave_u, c, first // PACK, how)
-                        at(clock(step + 1) + 0.3, quantize_u, c, first // PACK)
-                    else:
-                        at(clock(step) + W_S, weave_u, c, first // PACK, how)
-                        at(clock(step + 1) + Q_S, quantize_u, c, first // PACK)
-                step = second[c] + e
-                at(clock(step - 1) + 0.05, matmul_t, c, first)
-                at(clock(step - 1) + 0.55, abs_z, c, first)
-                at(clock(step) + 0.4, powers_z, c, first)
-                if last:
-                    at(clock(step + 1) + 0.1, turn_square, c, 0, e, "t")
-                    at(clock(step + 1) + (0.15 if e == 0 else 0.08), add_cubes, c, 0, first, per_bank)
-            done = second[c] + units[c]
-            for t in range(tiles):
-                now = clock(done + t)
-                how = ROUND[starts[c] // P + t]
-                if not last:
-                    at(now + D_CUBE, add_cubes, c, t, 0, TILES)
-                at(now + D_NORM, norm, c, t)
-                for h in range(GROUPS):
-                    if not last:
-                        at(now + D_SQ, turn_square, c, t, h, "turn")
-                    if how == "split":
-                        at(now + D_OUT, finish_half, c, t, h, ["scalar", "vector"][h], True)
-                        at(now + D_OUT, store_rows, c, t, slice(h * BANK, (h + 1) * BANK))
-                        at(now + D_ROUND, turn_rows, c, t, h, 1)
-                        at(now + D_ROWS, empty_rows, c, t, h, 1, ["scalar", "vector"][h])
-                    else:
-                        at(now + D_OUT, finish_half, c, t, h, "scalar", how == "scalar")
-                if how != "split":
-                    at(now + D_OUT, store_rows, c, t, slice(0, K))
-                    if how != "scalar":
-                        at(now + D_ROUND, round_rows, c, t, how)
-                    at(now + D_ROWS, turn_rows, c, t, 0, GROUPS)
-                    at(now + D_EMPTY, empty_rows, c, t, 0, GROUPS, "scalar")
-            at(now + D_PLANES, store_planes, c)
-            if last:
-                at(now + D_PLANES, store_scales, 0, S, [nc.scalar, nc.sync])
 
-        def prepare_a(pair, h):
-            turn_a(pair, h)
-            empty_a(pair, h, "scalar")
-
-        def prepare_x(t):
-            turn_x(0, t)
-            empty_x(0, t, "scalar")
-
-        weave_a(0, 0, "vector")
-        prepare_a(0, 0)
-        prepare_a(1, 0)
-        quantize_a2(0, 0)
-        quantize_a1(0, 0)
-        weave_a(0, 1, "vector")
-        prepare_x(0)
-        prepare_a(0, 1)
-        quantize_a1(1, 0)
-        quantize_a2(0, 1)
-        prepare_x(1)
-        prepare_a(1, 1)
-        gains()
-        quantize_a1(0, 1)
-        weave_a(1, 0, "vector")
-        quantize_x(0)
-        prepare_a(2, 0)
-        quantize_a1(1, 1)
-        quantize_a2(1, 0)
-        at(-1.9, turn_a, 2, 1)
-        at(-1.0, empty_a, 2, 1, "scalar")
-        at(-0.9, weave_a, 1, 1, "vector")
-        at(-0.8, quantize_a1, 2, 0)
-        at(-0.7, quantize_a2, 1, 1)
-        at(0.9, quantize_a1, 2, 1)
+        weave_a(0, 0)
         for h in range(GROUPS):
-            at(0.1, turn_a, 3, h)
-            at(0.9, empty_a, 3, h, "scalar")
-            at(3.5, quantize_a1, 3, h)
-        at(4.3, turn_d)
-        at(5.5, empty_d)
+            turn_a(0, h)
+            if h == 0:
+                turn_a(1, h)
+            turn_x(h)
+            empty_x(h)
+        turn_a(1, 1)
+        quantize_a_m(0, 0)
+        quantize_a_k(0, 0)
+        weave_a(0, 1)
+        quantize_a_k(1, 0)
+        quantize_a_m(0, 1)
+        quantize_a_k(0, 1)
+        quantize_x(0)
+        quantize_a_k(1, 1)
+        weave_a(1, 0)
 
-        for time, number, call, args in sorted(plan, key=lambda entry: entry[:2]):
-            call(*args)
+        turn_x(2)
+        turn_x(3)
+        matmul_y(0, 0)
+        matmul_y(0, 1)
+        empty_x(2)
+        empty_x(3)
+        abs_y(0, 0)
+        abs_y(0, 1)
+        quantize_a_m(1, 0)
+        quantize_x(1)
+        turn_a(2, 0)
+        turn_a(2, 1)
+        matmul_y(1, 0)
+        abs_y(1, 0)
+        make_u(0, 0)
+        weave_a(1, 1)
+        turn_a(3, 0)
+        turn_a(3, 1)
+        make_u(0, 1)
+        quantize_a_k(2, 0)
+        quantize_a_k(2, 1)
+        matmul_y(1, 1)
+
+        matmul_y(0, 2)
+        abs_y(1, 1)
+        abs_y(0, 2)
+        make_u(1, 0)
+        quantize_a_k(3, 0)
+        quantize_a_k(3, 1)
+        turn_x(4)
+        matmul_y(0, 3)
+        turn_x(5)
+        empty_x(4)
+        turn_d()
+        abs_y(0, 3)
+        weave_u(0, 0, "vector")
+        make_u(1, 1)
+        make_u(0, 2)
+        quantize_a_m(1, 1)
+        make_u(0, 3)
+        matmul_y(1, 2)
+        matmul_y(1, 3)
+        empty_x(5)
+        empty_d()
+        abs_y(1, 2)
+        abs_y(1, 3)
+        quantize_x(2)
+        matmul_y(2, 0)
+        weave_u(0, 1, "vector")
+        quantize_u(0, 0)
+        quantize_u(0, 1)
+        matmul_t(0)
+        turn_x(6)
+        weave_u(1, 0, "scalar")
+        make_u(1, 2)
+        make_u(1, 3)
+        abs_y(2, 0)
+        abs_z(0)
+        empty_x(6)
+
+        last = TILES - 1
+        pairs = TILES // 2
+        piece_done = [sum(n * TILES // BANK for n in PIECES[: q + 1]) for q in range(len(PIECES))]
+        ready = [piece_done[piece_of[t]] + t - piece_start[piece_of[t]] // P for t in range(last)]
+        for step in range(len(units)):
+            c, pair = 2 + step // pairs, step % pairs
+            c_next, pair_next = 2 + (step + 1) // pairs, (step + 1) % pairs
+            summed, stored, to_round, to_turn, to_quantize = [
+                [t for t in range(last) if ready[t] + lag == step] for lag in range(5)
+            ]
+
+            if c_next < CHUNKS:
+                matmul_y(c_next, pair_next)
+            if step + 1 < len(units):
+                matmul_t(step + 1)
+            if step == 0:
+                turn_x(last)
+            for t in summed:
+                add_cubes(t, 0, TILES, "turn" if c < CHUNKS else "y")
+            if step + 1 == len(units):
+                add_cubes(last, 0, PACK, "y")
+            for t in to_turn:
+                turn_rounded(t, "turn")
+            for t in stored:
+                turn_square(t, "turn")
+
+            if c_next < CHUNKS:
+                abs_y(c_next, pair_next)
+            if step + 1 < len(units):
+                abs_z(step + 1)
+            if pair == 0 and c <= CHUNKS:
+                weave_u(c - 1, 1, "scalar")
+            if pair == 2 and c < CHUNKS:
+                weave_u(c, 0, "scalar")
+            if step == 0:
+                empty_x(last)
+            for t in summed:
+                norm(t)
+            for t in to_turn:
+                empty_rounded(t, "scalar")
+            for t in stored:
+                if t < last - 1:
+                    store_result(t, ["scalar", "scalar"])
+
+            if c < CHUNKS:
+                make_u(c, pair)
+            powers_z(step)
+            if step == 0:
+                quantize_u(1, 0)
+            if pair == 1 and c <= CHUNKS:
+                quantize_u(c - 1, 1)
+            if pair == 3 and c < CHUNKS:
+                quantize_u(c, 0)
+            if step == 1:
+                quantize_x(CHUNKS - 1)
+            for t in to_round:
+                round_result(t)
+            for t in to_quantize:
+                if t % 2 == 1:
+                    store_codes(piece_of[t])
+
+        add_cubes(last, PACK, PACK, "y")
+        norm(last)
+        round_from_psum(last - 1, ["vector", "vector"])
+        turn_rounded(last - 2, "turn")
+        store_result(last - 1, ["scalar", "scalar"])
+        turn_square(last, "t")
+        turn_rounded(last - 1, "turn")
+        empty_rounded(last - 2, "vector")
+        round_from_psum(last, ["vector", "scalar"])
+        turn_rounded(last, "y")
+        empty_rounded(last - 1, "scalar")
+        store_result(last, ["vector", "scalar"])
+        store_codes(piece_of[last - 2])
+        empty_rounded(last, "scalar")
+        store_codes(piece_of[last - 1])
+        store_codes(piece_of[last])
+        store_scales()

@@ -25,6 +25,7 @@ EPS = 1e-6
 CHUNK = 256
 CHUNKS = S // CHUNK
 PIECES = [256, 256, 256, 128, 128]
+SCALAR_SHARE = 128
 BANKS = {"y": 3, "t": 2, "turn": 3}
 
 
@@ -91,8 +92,8 @@ def tile_weightedsignedsquarepowerstep_kernel(tc, x, a, w, d, out_0, out_1, out_
             nc.sync.dma_start(out=x_sb[t][:], in_=x[part(t, P), :])
 
         for h in range(GROUPS):
-            load_a(0, h)
             load_x(h)
+            load_a(0, h)
         for h in range(GROUPS):
             load_a(1, h)
         nc.sync.dma_start(
@@ -132,11 +133,11 @@ def tile_weightedsignedsquarepowerstep_kernel(tc, x, a, w, d, out_0, out_1, out_
                 turned[key][:].rearrange("p (b u r) -> p b r u", b=2, u=2),
             )
 
-        def weave(engine, out, in_):
+        def weave(engine, out, in_, cols):
             copy_on(
                 engine,
-                out.rearrange("p (c i j) -> p c j i", i=4, j=PACK),
-                in_.rearrange("p (j c i) -> p c j i", i=4, j=PACK),
+                out[:, PACK * cols.start : PACK * cols.stop].rearrange("p (c i j) -> p c j i", i=4, j=PACK),
+                in_[:].rearrange("p (j n) -> p j n", j=PACK)[:, :, cols].rearrange("p j (c i) -> p c j i", i=4),
             )
 
         def turn_d():
@@ -173,9 +174,10 @@ def tile_weightedsignedsquarepowerstep_kernel(tc, x, a, w, d, out_0, out_1, out_
         a_m = [mx_tiles(keep, "a_m%d" % g, K, 1) for g in range(GROUPS)]
         a_m_in = {}
 
-        def weave_a(g, h):
-            a_m_in[g, h] = work.tile([P, BANK * PACK], BF16, name="a_m_in", align_bytes=64)
-            weave("vector", a_m_in[g, h][:], a_sb[g, h][:])
+        def weave_a(g, h, engine, cols):
+            if (g, h) not in a_m_in:
+                a_m_in[g, h] = work.tile([P, BANK * PACK], BF16, name="a_m_in", align_bytes=64, bufs=3)
+            weave(engine, a_m_in[g, h], a_sb[g, h], cols)
 
         def quantize_a_m(g, h):
             quantize(a_m[g], part(h, BANK), a_m_in[g, h][:])
@@ -209,7 +211,7 @@ def tile_weightedsignedsquarepowerstep_kernel(tc, x, a, w, d, out_0, out_1, out_
 
         def weave_u(c, g, engine):
             u_in[c, g] = work.tile([P, CHUNK * PACK], BF16, name="u_in", align_bytes=64, bufs=3)
-            weave(engine, u_in[c, g][:], u_slots[c, g][:])
+            weave(engine, u_in[c, g], u_slots[c, g], slice(0, CHUNK))
 
         def quantize_u(c, g):
             u_m[c, g] = mx_tiles(keep, "u_m%d%d" % (c, g), CHUNK, 1)
@@ -356,23 +358,26 @@ def tile_weightedsignedsquarepowerstep_kernel(tc, x, a, w, d, out_0, out_1, out_
                 )
 
 
-        weave_a(0, 0)
-        for h in range(GROUPS):
-            turn_a(0, h)
-            if h == 0:
-                turn_a(1, h)
-            turn_x(h)
-            empty_x(h)
+        whole, shared, rest = slice(0, BANK), slice(0, SCALAR_SHARE), slice(SCALAR_SHARE, BANK)
+        weave_a(0, 0, "vector", whole)
+        turn_x(0)
+        empty_x(0)
+        turn_a(0, 0)
+        turn_a(1, 0)
+        turn_x(1)
+        empty_x(1)
+        turn_a(0, 1)
         turn_a(1, 1)
+        weave_a(1, 0, "scalar", shared)
         quantize_a_m(0, 0)
         quantize_a_k(0, 0)
-        weave_a(0, 1)
+        weave_a(0, 1, "vector", whole)
         quantize_a_k(1, 0)
         quantize_a_m(0, 1)
         quantize_a_k(0, 1)
         quantize_x(0)
         quantize_a_k(1, 1)
-        weave_a(1, 0)
+        weave_a(1, 0, "vector", rest)
 
         turn_x(2)
         turn_x(3)
@@ -380,6 +385,7 @@ def tile_weightedsignedsquarepowerstep_kernel(tc, x, a, w, d, out_0, out_1, out_
         matmul_y(0, 1)
         empty_x(2)
         empty_x(3)
+        weave_a(1, 1, "scalar", shared)
         abs_y(0, 0)
         abs_y(0, 1)
         quantize_a_m(1, 0)
@@ -389,7 +395,7 @@ def tile_weightedsignedsquarepowerstep_kernel(tc, x, a, w, d, out_0, out_1, out_
         matmul_y(1, 0)
         abs_y(1, 0)
         make_u(0, 0)
-        weave_a(1, 1)
+        weave_a(1, 1, "vector", rest)
         turn_a(3, 0)
         turn_a(3, 1)
         make_u(0, 1)
@@ -444,6 +450,7 @@ def tile_weightedsignedsquarepowerstep_kernel(tc, x, a, w, d, out_0, out_1, out_
             summed, stored, to_round, to_turn, to_quantize = [
                 [t for t in range(last) if ready[t] + lag == step] for lag in range(5)
             ]
+            spare = "turn" if c < CHUNKS else "y"
 
             if c_next < CHUNKS:
                 matmul_y(c_next, pair_next)
@@ -452,11 +459,11 @@ def tile_weightedsignedsquarepowerstep_kernel(tc, x, a, w, d, out_0, out_1, out_
             if step == 0:
                 turn_x(last)
             for t in summed:
-                add_cubes(t, 0, TILES, "turn" if c < CHUNKS else "y")
+                add_cubes(t, 0, TILES, spare)
             if step + 1 == len(units):
-                add_cubes(last, 0, PACK, "y")
+                add_cubes(last, 0, PACK, spare)
             for t in to_turn:
-                turn_rounded(t, "turn")
+                turn_rounded(t, spare)
             for t in stored:
                 turn_square(t, "turn")
 
@@ -466,7 +473,7 @@ def tile_weightedsignedsquarepowerstep_kernel(tc, x, a, w, d, out_0, out_1, out_
                 abs_z(step + 1)
             if pair == 0 and c <= CHUNKS:
                 weave_u(c - 1, 1, "scalar")
-            if pair == 2 and c < CHUNKS:
+            if pair == 2 and c < CHUNKS - 1:
                 weave_u(c, 0, "scalar")
             if step == 0:
                 empty_x(last)
@@ -481,6 +488,8 @@ def tile_weightedsignedsquarepowerstep_kernel(tc, x, a, w, d, out_0, out_1, out_
             if c < CHUNKS:
                 make_u(c, pair)
             powers_z(step)
+            if pair == 1 and c == CHUNKS - 1:
+                weave_u(c, 0, "vector")
             if step == 0:
                 quantize_u(1, 0)
             if pair == 1 and c <= CHUNKS:
@@ -498,15 +507,15 @@ def tile_weightedsignedsquarepowerstep_kernel(tc, x, a, w, d, out_0, out_1, out_
         add_cubes(last, PACK, PACK, "y")
         norm(last)
         round_from_psum(last - 1, ["vector", "vector"])
+        turn_square(last, "t")
         turn_rounded(last - 2, "turn")
         store_result(last - 1, ["scalar", "scalar"])
-        turn_square(last, "t")
         turn_rounded(last - 1, "turn")
-        empty_rounded(last - 2, "vector")
         round_from_psum(last, ["vector", "scalar"])
         turn_rounded(last, "y")
-        empty_rounded(last - 1, "scalar")
         store_result(last, ["vector", "scalar"])
+        empty_rounded(last - 2, "vector")
+        empty_rounded(last - 1, "scalar")
         store_codes(piece_of[last - 2])
         empty_rounded(last, "scalar")
         store_codes(piece_of[last - 1])

from contextlib import ExitStack

import concourse.mybir as mybir
from concourse.masks import make_identity

S, K, M = 1024, 1024, 1024
FLOPS = 2 * S * K * M * 2

F32 = mybir.dt.float32
BF16 = mybir.dt.bfloat16
U32 = mybir.dt.uint32
I32 = mybir.dt.int32
U8 = mybir.dt.uint8
FP8X4 = mybir.dt.float8_e4m3fn_x4
ACT = mybir.ActivationFunctionType
ALU = mybir.AluOpType

P = 128
PACK = 4
BANK = 512
GROUPS = 2
TILES = 8
EPS = 1e-6

CHUNK = 256
CHUNKS = S // CHUNK
PIECES = [256, 256, 256, 128, 128]
SCALAR_SHARE = 128
BANKS = {"y": 3, "t": 2, "turn": 3}


def tile_weightedsignedsquarepowerstep_kernel(tc, x, a, w, d, out_0, out_1, out_2):
    nc = tc.nc

    with ExitStack() as ctx:
        keep = ctx.enter_context(tc.tile_pool(name="keep", bufs=1))
        work = ctx.enter_context(tc.tile_pool(name="work", bufs=2))
        psum = ctx.enter_context(tc.psum_pool(name="psum", bufs=1))
        ctx.enter_context(tc.manual_schedule())

        def new_bank(role):
            return psum.tile([P, BANK], F32, name=role, bufs=BANKS[role])

        def copy_on(engine, out, in_):
            if engine == "scalar":
                nc.scalar.copy(out=out, in_=in_)
            else:
                nc.vector.tensor_copy(out=out, in_=in_)

        def scale_on(engine, out, in_, factor):
            if engine == "scalar":
                nc.scalar.activation(out=out, in_=in_, func=ACT.Copy, scale=factor)
            else:
                nc.vector.tensor_scalar(out=out, in0=in_, scalar1=factor, scalar2=None, op0=ALU.mult)

        def mx_tiles(pool, name, words, bufs):
            codes = pool.tile([P, words], U32, name=name + "_codes", align_bytes=64, bufs=bufs)
            scales = pool.tile([P, words], U8, name=name + "_scales", align_bytes=64, bufs=bufs)
            return codes, scales

        def quantize(operand, cols, values):
            nc.vector.quantize_mx(out=operand[0][:, cols].bitcast(FP8X4), scales=operand[1][:, cols], in_=values)

        def mx_product(out, passes):
            for g, (left, left_cols, right, right_cols) in enumerate(passes):
                nc.tensor.matmul_mx(
                    out=out,
                    lhsT=left[0][:, left_cols].bitcast(FP8X4),
                    lhsT_scale=left[1][:, left_cols],
                    rhs=right[0][:, right_cols].bitcast(FP8X4),
                    rhs_scale=right[1][:, right_cols],
                    start=(g == 0),
                    stop=(g == GROUPS - 1),
                )

        def part(index, width):
            return slice(index * width, (index + 1) * width)

        a_parts = a.rearrange("(g p j) (h c) -> g h p j c", g=GROUPS, j=PACK, h=GROUPS)
        a_sb = {}
        for g in range(GROUPS):
            for h in range(GROUPS):
                a_sb[g, h] = keep.tile([P, PACK * BANK], BF16, name="a_sb%d%d" % (g, h), align_bytes=256)
        x_sb = [keep.tile([P, K], BF16, name="x_sb%d" % t, align_bytes=256) for t in range(TILES)]
        w_col = keep.tile([P, TILES], BF16, name="w_col")
        d_rows = keep.tile([TILES, P], BF16, name="d_rows")

        def load_a(g, h):
            nc.sync.dma_start(out=a_sb[g, h][:].rearrange("p (j c) -> p j c", j=PACK), in_=a_parts[g][h])

        def load_x(t):
            nc.sync.dma_start(out=x_sb[t][:], in_=x[part(t, P), :])

        for h in range(GROUPS):
            load_x(h)
            load_a(0, h)
        for h in range(GROUPS):
            load_a(1, h)
        nc.sync.dma_start(
            out=w_col[:].rearrange("p (g j) -> p g j", j=PACK),
            in_=w.rearrange("(g p j) -> p g j", g=GROUPS, j=PACK),
        )
        load_x(2)
        load_x(3)
        nc.sync.dma_start(out=d_rows[:], in_=d.rearrange("(i p) -> i p", p=P))
        for t in range(4, TILES):
            load_x(t)

        ident = keep.tile([P, P], F32, name="ident")
        make_identity(nc, ident[:])
        one = keep.tile([P, 1], F32, name="one")
        nc.vector.memset(one[:], 1.0)
        power = keep.tile([P, 1], F32, name="power")
        nc.scalar.activation(out=power[:], in_=one[:], func=ACT.Identity, scale=-2.0 / 3.0)
        d_square = keep.tile([P, P], F32, name="d_square")
        nc.gpsimd.memset(d_square[:], 0.0)
        d_col = keep.tile([P, TILES], F32, name="d_col")

        turned = {}

        def turn(key, sources, role):
            turned[key] = new_bank(role)
            for e, source in enumerate(sources):
                nc.tensor.transpose(turned[key][:, part(e, P)], source, ident[:])

        def every_second(words):
            return [words[:, 2 * P * b + u : 2 * P * (b + 1) : 2] for b in range(2) for u in range(2)]

        def empty_words(key, engine, staged, rows):
            copy_on(
                engine,
                staged[:].bitcast(F32).rearrange("p (b r u) -> p b r u", b=2, u=2)[:, :, rows, :],
                turned[key][:].rearrange("p (b u r) -> p b r u", b=2, u=2),
            )

        def weave(engine, out, in_, cols):
            copy_on(
                engine,
                out[:, PACK * cols.start : PACK * cols.stop].rearrange("p (c i j) -> p c j i", i=4, j=PACK),
                in_[:].rearrange("p (j n) -> p j n", j=PACK)[:, :, cols].rearrange("p j (c i) -> p c j i", i=4),
            )

        def turn_d():
            nc.scalar.copy(out=d_square[0:TILES, :], in_=d_rows[:])
            turn("d", [d_square[:]], "turn")

        def empty_d():
            nc.scalar.copy(out=d_col[:], in_=turned["d"][:, 0:TILES])

        a_k = [mx_tiles(keep, "a_k%d" % pair, GROUPS * 2 * P, 1) for pair in range(TILES // 2)]
        a_k_in, x_in, x_k = {}, {}, {}

        def turn_a(pair, h):
            words = a_sb[pair // 2, h][:].bitcast(F32)
            turn(("a", pair, h), every_second(words[:, part(pair % 2, BANK)]), "turn")
            a_k_in[pair, h] = work.tile([P, 2 * P * PACK], BF16, name="a_k_in", align_bytes=64, bufs=4)
            empty_words(("a", pair, h), "scalar", a_k_in[pair, h], slice(0, P))

        def quantize_a_k(pair, h):
            quantize(a_k[pair], part(h, 2 * P), a_k_in[pair, h][:])

        def turn_x(t):
            turn(("x", t), every_second(x_sb[t][:].bitcast(F32)), "turn")

        def empty_x(t):
            if t % 2 == 0:
                x_in[t // 2] = work.tile([P, GROUPS * CHUNK * PACK], BF16, name="x_in", align_bytes=64)
            empty_words(("x", t), "scalar", x_in[t // 2], part(t % 2, P))

        def quantize_x(c):
            x_k[c] = mx_tiles(keep, "x_k%d" % c, GROUPS * CHUNK, 1)
            quantize(x_k[c], slice(0, GROUPS * CHUNK), x_in[c][:])

        a_m = [mx_tiles(keep, "a_m%d" % g, K, 1) for g in range(GROUPS)]
        a_m_in = {}

        def weave_a(g, h, engine, cols):
            if (g, h) not in a_m_in:
                a_m_in[g, h] = work.tile([P, BANK * PACK], BF16, name="a_m_in", align_bytes=64, bufs=3)
            weave(engine, a_m_in[g, h], a_sb[g, h], cols)

        def quantize_a_m(g, h):
            quantize(a_m[g], part(h, BANK), a_m_in[g, h][:])

        y_bank, y_abs, u_slots, u_in, u_m = {}, {}, {}, {}, {}

        def matmul_y(c, pair):
            y_bank[c, pair] = new_bank("y")
            for e in range(2):
                passes = [(a_k[pair], part(2 * h + e, P), x_k[c], part(h, CHUNK)) for h in range(GROUPS)]
                mx_product(y_bank[c, pair][:, part(e, CHUNK)], passes)

        def abs_y(c, pair):
            y_abs[c, pair] = work.tile([P, BANK], F32, name="y_abs", bufs=BANKS["y"] + 1)
            nc.scalar.activation(out=y_abs[c, pair][:], in_=y_bank[c, pair][:], func=ACT.Abs)

        def make_u(c, pair):
            g = pair // 2
            if pair % 2 == 0:
                u_slots[c, g] = work.tile([P, PACK * CHUNK], BF16, name="u_slots", bufs=3)
            for e in range(2):
                i = 2 * pair + e
                nc.vector.scalar_tensor_tensor(
                    out=u_slots[c, g][:, part(i % PACK, CHUNK)],
                    in0=y_bank[c, pair][:, part(e, CHUNK)],
                    scalar=w_col[:, i : i + 1],
                    in1=y_abs[c, pair][:, part(e, CHUNK)],
                    op0=ALU.mult,
                    op1=ALU.mult,
                )

        def weave_u(c, g, engine):
            u_in[c, g] = work.tile([P, CHUNK * PACK], BF16, name="u_in", align_bytes=64, bufs=3)
            weave(engine, u_in[c, g], u_slots[c, g], slice(0, CHUNK))

        def quantize_u(c, g):
            u_m[c, g] = mx_tiles(keep, "u_m%d%d" % (c, g), CHUNK, 1)
            quantize(u_m[c, g], slice(0, CHUNK), u_in[c, g][:])

        piece_start = [sum(PIECES[:q]) for q in range(len(PIECES))]
        units = [(q, first) for q, n in enumerate(PIECES) for first in range(0, TILES, BANK // n)]
        piece_of = [q for q, n in enumerate(PIECES) for t in range(n // P)]
        t_bank, z_abs, square, cube = {}, {}, {}, {}

        def matmul_t(unit):
            q, first = units[unit]
            n, c, row = PIECES[q], piece_start[q] // CHUNK, piece_start[q] % CHUNK
            t_bank[unit] = new_bank("t")
            for e in range(BANK // n):
                passes = [(a_m[g], part(first + e, P), u_m[c, g], slice(row, row + n)) for g in range(GROUPS)]
                mx_product(t_bank[unit][:, part(e, n)], passes)

        def abs_z(unit):
            q, first = units[unit]
            n = PIECES[q]
            z_abs[unit] = work.tile([P, BANK], F32, name="z_abs")
            for e in range(BANK // n):
                nc.scalar.activation(
                    out=z_abs[unit][:, part(e, n)],
                    in_=t_bank[unit][:, part(e, n)],
                    func=ACT.Abs,
                    scale=d_col[:, first + e : first + e + 1],
                )

        def times_z(unit, out, factor):
            q, first = units[unit]
            n = PIECES[q]
            for e in range(BANK // n):
                nc.vector.scalar_tensor_tensor(
                    out=out[:, part(e, n)],
                    in0=t_bank[unit][:, part(e, n)],
                    scalar=d_col[:, first + e : first + e + 1],
                    in1=factor[:, part(e, n)],
                    op0=ALU.mult,
                    op1=ALU.mult,
                )

        def powers_z(unit):
            q, first = units[unit]
            n = PIECES[q]
            if first == 0:
                square[q] = work.tile([P, TILES * n], F32, name="square", bufs=3)
                cube[q] = work.tile([P, TILES * n], F32, name="cube")
            cols = slice(first * n, first * n + BANK)
            times_z(unit, square[q][:, cols], z_abs[unit][:])
            times_z(unit, cube[q][:, cols], square[q][:, cols])

        def block(values, t, i):
            q = piece_of[t]
            start = i * PIECES[q] + t * P - piece_start[q]
            return values[q][:, start : start + P]

        inv_norm = {}

        def add_cubes(t, first, count, role):
            if first == 0:
                turned["cube", t] = new_bank(role)
            for i in range(first, first + count):
                nc.tensor.matmul(
                    out=turned["cube", t][:, 0:P],
                    lhsT=block(cube, t, i),
                    rhs=ident[:],
                    start=(i == 0),
                    stop=(i == TILES - 1),
                    is_transpose=True,
                )

        def norm(t):
            terms = work.tile([P, P], F32, name="terms")
            mean = work.tile([P, 1], F32, name="mean")
            nc.scalar.activation(
                out=terms[:],
                in_=turned["cube", t][:, 0:P],
                func=ACT.Identity,
                scale=1.0 / K,
                bias=EPS / P,
                accum_out=mean[:],
            )
            inv_norm[t] = work.tile([P, 1], F32, name="inv_norm", bufs=3)
            nc.gpsimd.tensor_tensor(out=inv_norm[t][:], in0=mean[:], in1=power[:], op=ALU.pow)

        result, rounded, out_in = {}, {}, {}
        out_k = mx_tiles(keep, "out_k", GROUPS * S, 1)

        def turn_square(t, role):
            for h in range(GROUPS):
                turn(("square", t, h), [block(square, t, h * PACK + e) for e in range(PACK)], role)

        def store_result(t, engines):
            result[t] = work.tile([P, K], F32, name="result", bufs=3, align_bytes=256)
            for h in range(GROUPS):
                scale_on(engines[h], result[t][:, part(h, BANK)], turned["square", t, h][:], inv_norm[t][:])
            nc.sync.dma_start(out=out_0[part(t, P), :], in_=result[t][:])

        def round_result(t):
            rounded[t] = work.tile([P, K], BF16, name="rounded")
            nc.vector.tensor_copy(
                out=rounded[t][:].rearrange("p (h u r e) -> p h u r e", h=GROUPS, u=2, e=2),
                in_=result[t][:].rearrange("p (h r u e) -> p h u r e", h=GROUPS, u=2, e=2),
            )

        def round_from_psum(t, engines):
            rounded[t] = work.tile([P, K], BF16, name="rounded")
            for h in range(GROUPS):
                scale_on(
                    engines[h],
                    rounded[t][:, part(h, BANK)].rearrange("p (u r e) -> p u r e", u=2, e=2),
                    turned["square", t, h][:].rearrange("p (r u e) -> p u r e", u=2, e=2),
                    inv_norm[t][:],
                )

        def turn_rounded(t, role):
            words = rounded[t][:].bitcast(F32)
            turn(("rounded", t), [words[:, part(e, P)] for e in range(2 * GROUPS)], role)

        def empty_rounded(t, engine):
            q = piece_of[t]
            row = t * P - piece_start[q]
            if row == 0:
                out_in[q] = work.tile([P, GROUPS * PIECES[q] * PACK], BF16, name="out_in", align_bytes=64, bufs=3)
            empty_words(("rounded", t), engine, out_in[q], slice(row, row + P))

        def store_codes(q):
            rows = slice(piece_start[q], piece_start[q] + PIECES[q])
            for h in range(GROUPS):
                quantize(out_k, slice(h * S + rows.start, h * S + rows.stop), out_in[q][:, part(h, PIECES[q] * PACK)])
            nc.sync.dma_start(
                out=out_1.rearrange("h p s j -> p h (s j)").bitcast(I32)[:, :, rows],
                in_=out_k[0][:].bitcast(I32).rearrange("p (h s) -> p h s", h=GROUPS)[:, :, rows],
            )

        def store_scales():
            for quad in range(4):
                queue = nc.scalar if quad % 2 == 0 else nc.sync
                queue.dma_start(
                    out=out_2.bitcast(I32)[:, part(quad, 4), :].rearrange("h r s -> r h s"),
                    in_=out_k[1][32 * quad : 32 * quad + 4, :].bitcast(I32).rearrange("p (h s) -> p h s", h=GROUPS),
                )


        whole, shared, rest = slice(0, BANK), slice(0, SCALAR_SHARE), slice(SCALAR_SHARE, BANK)
        weave_a(0, 0, "vector", whole)
        turn_x(0)
        empty_x(0)
        turn_a(0, 0)
        turn_a(1, 0)
        turn_x(1)
        empty_x(1)
        turn_a(0, 1)
        turn_a(1, 1)
        weave_a(1, 0, "scalar", shared)
        quantize_a_m(0, 0)
        quantize_a_k(0, 0)
        weave_a(0, 1, "vector", whole)
        quantize_a_k(1, 0)
        quantize_a_m(0, 1)
        quantize_a_k(0, 1)
        quantize_x(0)
        quantize_a_k(1, 1)
        weave_a(1, 0, "vector", rest)

        turn_x(2)
        turn_x(3)
        matmul_y(0, 0)
        matmul_y(0, 1)
        empty_x(2)
        empty_x(3)
        weave_a(1, 1, "scalar", shared)
        abs_y(0, 0)
        abs_y(0, 1)
        quantize_a_m(1, 0)
        quantize_x(1)
        turn_a(2, 0)
        turn_a(2, 1)
        matmul_y(1, 0)
        abs_y(1, 0)
        make_u(0, 0)
        weave_a(1, 1, "vector", rest)
        turn_a(3, 0)
        turn_a(3, 1)
        make_u(0, 1)
        quantize_a_k(2, 0)
        quantize_a_k(2, 1)
        matmul_y(1, 1)

        matmul_y(0, 2)
        abs_y(1, 1)
        abs_y(0, 2)
        make_u(1, 0)
        quantize_a_k(3, 0)
        quantize_a_k(3, 1)
        turn_x(4)
        matmul_y(0, 3)
        turn_x(5)
        empty_x(4)
        turn_d()
        abs_y(0, 3)
        weave_u(0, 0, "vector")
        make_u(1, 1)
        make_u(0, 2)
        quantize_a_m(1, 1)
        make_u(0, 3)
        matmul_y(1, 2)
        matmul_y(1, 3)
        empty_x(5)
        empty_d()
        abs_y(1, 2)
        abs_y(1, 3)
        quantize_x(2)
        matmul_y(2, 0)
        weave_u(0, 1, "vector")
        quantize_u(0, 0)
        quantize_u(0, 1)
        matmul_t(0)
        turn_x(6)
        weave_u(1, 0, "scalar")
        make_u(1, 2)
        make_u(1, 3)
        abs_y(2, 0)
        abs_z(0)
        empty_x(6)

        last = TILES - 1
        pairs = TILES // 2
        piece_done = [sum(n * TILES // BANK for n in PIECES[: q + 1]) for q in range(len(PIECES))]
        ready = [piece_done[piece_of[t]] + t - piece_start[piece_of[t]] // P for t in range(last)]
        for step in range(len(units)):
            c, pair = 2 + step // pairs, step % pairs
            c_next, pair_next = 2 + (step + 1) // pairs, (step + 1) % pairs
            summed, stored, to_round, to_turn, to_quantize = [
                [t for t in range(last) if ready[t] + lag == step] for lag in range(5)
            ]
            spare = "turn" if c < CHUNKS else "y"

            if c_next < CHUNKS:
                matmul_y(c_next, pair_next)
            if step + 1 < len(units):
                matmul_t(step + 1)
            if step == 0:
                turn_x(last)
            for t in summed:
                add_cubes(t, 0, TILES, spare)
            if step + 1 == len(units):
                add_cubes(last, 0, PACK, spare)
            for t in to_turn:
                turn_rounded(t, spare)
            for t in stored:
                turn_square(t, "turn")

            if c_next < CHUNKS:
                abs_y(c_next, pair_next)
            if step + 1 < len(units):
                abs_z(step + 1)
            if pair == 0 and c <= CHUNKS:
                weave_u(c - 1, 1, "scalar")
            if pair == 2 and c < CHUNKS - 1:
                weave_u(c, 0, "scalar")
            if step == 0:
                empty_x(last)
            for t in summed:
                norm(t)
            for t in to_turn:
                empty_rounded(t, "scalar")
            for t in stored:
                if t < last - 1:
                    store_result(t, ["scalar", "scalar"])

            if c < CHUNKS:
                make_u(c, pair)
            powers_z(step)
            if pair == 1 and c == CHUNKS - 1:
                weave_u(c, 0, "vector")
            if step == 0:
                quantize_u(1, 0)
            if pair == 1 and c <= CHUNKS:
                quantize_u(c - 1, 1)
            if pair == 3 and c < CHUNKS:
                quantize_u(c, 0)
            if step == 1:
                quantize_x(CHUNKS - 1)
            for t in to_round:
                round_result(t)
            for t in to_quantize:
                if t % 2 == 1:
                    store_codes(piece_of[t])

        add_cubes(last, PACK, PACK, "y")
        norm(last)
        round_from_psum(last - 1, ["vector", "vector"])
        turn_square(last, "t")
        turn_rounded(last - 2, "turn")
        store_result(last - 1, ["scalar", "scalar"])
        turn_rounded(last - 1, "turn")
        round_from_psum(last, ["vector", "scalar"])
        turn_rounded(last, "y")
        store_result(last, ["vector", "scalar"])
        empty_rounded(last - 2, "vector")
        empty_rounded(last - 1, "scalar")
        store_codes(piece_of[last - 2])
        empty_rounded(last, "scalar")
        store_codes(piece_of[last - 1])
        store_codes(piece_of[last])
        store_scales()
